import numpy as np
import ml_dtypes


def mxq(x, axis, fmt="e4m3"):
    dtype, down = {"e4m3": (ml_dtypes.float8_e4m3fn, 7), "e5m2": (ml_dtypes.float8_e5m2, 14)}[fmt]
    v = np.moveaxis(np.asarray(x, np.float32).astype(ml_dtypes.bfloat16).astype(np.float64), axis, -1)
    blocks = v.reshape(v.shape[:-1] + (-1, 32))
    amax = np.abs(blocks).max(-1, keepdims=True)
    byte = np.maximum(np.where(amax > 0, np.frexp(amax)[1] - 1 + 127, 0) - down, 1)
    scale = np.exp2(byte - 127.0)
    codes = (blocks / scale).astype(np.float32).astype(dtype).astype(np.float64)
    return np.moveaxis((codes * scale).reshape(v.shape), -1, axis)


WIDE = False


def mx_kscale(k):
    if not WIDE:
        return np.ones(k)
    levels = np.array([10, -10, 5, -5, 0])
    if k % 512:
        return np.exp2(np.random.permutation(np.resize(levels, k // 32))).repeat(32)
    a = np.empty((k // 512, 16))
    for p in range(k // 512):
        a[p, :8] = np.random.permutation(np.resize(levels, 8))
        for g in range(8):
            far = levels[np.abs(levels - a[p, g]) >= 10]
            a[p, g + 8] = far[np.random.randint(len(far))]
    return np.exp2(a.ravel()).repeat(32)


def f64(x):
    return np.asarray(x).astype(np.float64)


def striped(idx):
    return np.tile(np.asarray(idx).reshape(-1, 16).T, (8, 1)).astype(np.uint16)


def unstriped(offs):
    return offs[:16].T.reshape(-1).astype(np.int64)


E2M1 = np.array([0.0, 0.5, 1.0, 1.5, 2.0, 3.0, 4.0, 6.0, -0.0, -0.5, -1.0, -1.5, -2.0, -3.0, -4.0, -6.0])


def pack_weight(w, fmt):
    k, n = w.shape
    w = f64(np.asarray(w, np.float32).astype(ml_dtypes.bfloat16)).reshape(k // 32, 32, n)
    amax = np.abs(w).max(1)
    if fmt == "e4m3":
        byte = np.frexp(amax)[1] - 1 + 127 - 7
    else:
        mant, ex = np.frexp(amax / 6.0)
        byte = np.where(mant > 0.5, ex, ex - 1) + 127
    byte = np.clip(np.where(amax > 0, byte, 1), 1, 254)
    scaled = (w * np.exp2(127.0 - byte)[:, None, :]).reshape(k, n).astype(np.float32)
    by_word = np.ascontiguousarray(scaled.reshape(k // 512, 128, 4, n).transpose(0, 1, 3, 2))
    if fmt == "e4m3":
        words = by_word.astype(ml_dtypes.float8_e4m3fn).view(np.uint8)
    else:
        c = by_word.astype(ml_dtypes.float4_e2m1fn).view(np.uint8) & 0xF
        words = (c[..., 0::2] | (c[..., 1::2] << 4)).reshape(k // 512, 128, 2 * n)
    return np.ascontiguousarray(words), np.ascontiguousarray(byte.astype(np.uint8).reshape(k // 512, 16, n))


def unpack_weight(words, scales, fmt):
    g, _, n = scales.shape
    words = np.ascontiguousarray(words).reshape(g, 128, n, -1)
    if fmt == "e4m3":
        vals = words.view(ml_dtypes.float8_e4m3fn).astype(np.float64)
    else:
        nib = np.empty((g, 128, n, 4), np.uint8)
        nib[..., 0::2] = words & 0xF
        nib[..., 1::2] = words >> 4
        vals = E2M1[nib]
    vals = vals * np.repeat(np.exp2(scales.astype(np.float64) - 127.0), 8, axis=1)[..., None]
    return vals.transpose(0, 1, 3, 2).reshape(g * 512, n)


def bf(x):
    return np.asarray(x, np.float32).astype(ml_dtypes.bfloat16)


def planes(Y):
    r, m = Y.shape
    b = f64(bf(Y)).reshape(r // 32, 32, m)
    amax = np.abs(b).max(1)
    byte = np.clip(np.where(amax > 0, np.frexp(amax)[1] - 1 + 127 - 7, 1), 1, 254)
    codes = (b * np.exp2(127.0 - byte)[:, None, :]).reshape(r, m).astype(np.float32).astype(ml_dtypes.float8_e4m3fn).view(np.uint8)
    words = codes.reshape(r // 512, 128, 4, m).transpose(0, 1, 3, 2)
    return np.ascontiguousarray(words), np.ascontiguousarray(byte.astype(np.uint8).reshape(r // 512, 16, m))


K, T, J, N = 512, 1024, 256, 512


def setup_inputs():
    n = np.random.standard_normal
    idx = np.random.permutation(T)[:J]
    idx2 = np.random.permutation(T)[:J]
    fk = mx_kscale(K)
    xqp = pack_weight(n((K, T)) / fk[:, None], "e2m1")
    wqp = pack_weight(n((K, N)) * 1 / np.sqrt(K) * fk[:, None], "e4m3")
    wfp = pack_weight(n((K, N)) * 1 / np.sqrt(K) * fk[:, None], "e2m1")
    return {
        "xq_words": xqp[0],
        "xq_scales": xqp[1],
        "wq_words": wqp[0],
        "wq_scales": wqp[1],
        "xf": (n((K, T)) / fk[:, None]).astype(np.float32),
        "wf_words": wfp[0],
        "wf_scales": wfp[1],
        "offs": striped(idx),
        "offs2": striped(idx2),
    }


def reference(xq_words, xq_scales, wq_words, wq_scales, xf, wf_words, wf_scales, offs, offs2):
    idx = unstriped(offs)
    idx2 = unstriped(offs2)
    xqu = unpack_weight(xq_words, xq_scales, "e2m1")
    wqu = unpack_weight(wq_words, wq_scales, "e4m3")
    wfu = unpack_weight(wf_words, wf_scales, "e2m1")
    z = wqu.T @ xqu
    d = f64(xf)[:, idx] - f64(xf)[:, idx2]
    dq = mxq(d, 0, "e4m3")
    p = wfu.T @ dq
    y = z[:, idx2] + p
    words, scales = planes(y)
    return y, words, scales

@@ -1,0 +1,157 @@
+from contextlib import ExitStack
+
+import concourse.mybir as mybir
+
+K, T, J, N = 512, 1024, 256, 512
+FLOPS = 2 * K * N * (T + J)
+
+F32 = mybir.dt.float32
+BF16 = mybir.dt.bfloat16
+I32 = mybir.dt.int32
+U32 = mybir.dt.uint32
+U16 = mybir.dt.uint16
+U8 = mybir.dt.uint8
+FP8X4 = mybir.dt.float8_e4m3fn_x4
+FP4X4 = mybir.dt.float4_e2m1fn_x4
+
+P = 128
+PACK = 4
+BANK = 512
+QUADS = 4
+
+
+def tile_list_change_since_lists_pl_kernel(
+    tc, xq_words, xq_scales, wq_words, wq_scales, xf, wf_words, wf_scales, offs, offs2, out_0, out_1, out_2
+):
+    nc = tc.nc
+    add, subtract = mybir.AluOpType.add, mybir.AluOpType.subtract
+
+    with ExitStack() as ctx:
+        lists = ctx.enter_context(tc.tile_pool(name="lists", bufs=1))
+        keep = ctx.enter_context(tc.tile_pool(name="keep", bufs=1))
+        z_psum = ctx.enter_context(tc.psum_pool(name="z_psum", bufs=6))
+        p_psum = ctx.enter_context(tc.psum_pool(name="p_psum", bufs=1))
+
+        def load_scale_rows(plane, rows):
+            for q in range(QUADS):
+                nc.scalar.dma_start(
+                    out=plane[32 * q : 32 * q + 4, :].bitcast(I32),
+                    in_=rows[0, 4 * q : 4 * q + 4, :].bitcast(I32),
+                )
+
+        wq_scale_raw = keep.tile([P, N], U8, align_bytes=64)
+        xq_scale = keep.tile([P, T], U8, align_bytes=64)
+        wf_scale_raw = keep.tile([P, N], U8, align_bytes=64)
+        nc.vector.memset(wq_scale_raw[:].bitcast(I32), 0)
+        nc.vector.memset(xq_scale[:].bitcast(I32), 0)
+        nc.vector.memset(wf_scale_raw[:].bitcast(I32), 0)
+
+        wq_raw = keep.tile([P, N], I32, align_bytes=64)
+        xq_codes = keep.tile([P, 2 * T], U8, align_bytes=64)
+        wf_raw = keep.tile([P, 2 * N], U8, align_bytes=64)
+        new_list = lists.tile([P, J // 16], U16)
+        old_list = lists.tile([P, J // 16], U16)
+        xf_planes = [keep.tile([P, T], F32, name="xf_plane%d" % t) for t in range(PACK)]
+        xf_rows = xf.rearrange("(p t) c -> p t c", t=PACK)
+
+        nc.sync.dma_start(out=wq_raw[:], in_=wq_words[0].rearrange("p n r -> p (n r)").bitcast(I32))
+        load_scale_rows(wq_scale_raw, wq_scales)
+        nc.sync.dma_start(out=xq_codes[:].bitcast(I32), in_=xq_words[0].bitcast(I32))
+        load_scale_rows(xq_scale, xq_scales)
+        nc.sync.dma_start(old_list[:], offs2)
+        nc.sync.dma_start(out=xf_planes[0][:], in_=xf_rows[:, 0, :])
+        nc.sync.dma_start(new_list[:], offs)
+        nc.sync.dma_start(out=xf_planes[1][:], in_=xf_rows[:, 1, :])
+        nc.sync.dma_start(out=wf_raw[:].bitcast(I32), in_=wf_words[0].bitcast(I32))
+        load_scale_rows(wf_scale_raw, wf_scales)
+        nc.sync.dma_start(out=xf_planes[2][:], in_=xf_rows[:, 2, :])
+        nc.sync.dma_start(out=xf_planes[3][:], in_=xf_rows[:, 3, :])
+
+        def deal(dealt, raw, run):
+            nc.vector.tensor_copy(
+                out=dealt.rearrange("p (t c i) -> p c t i", t=PACK, i=run),
+                in_=raw.rearrange("p (c i t) -> p c t i", t=PACK, i=run),
+            )
+
+        wq_codes = keep.tile([P, N], I32, align_bytes=64)
+        wq_scale = keep.tile([P, N], U8, align_bytes=64)
+        wf_codes = keep.tile([P, 2 * N], U8, align_bytes=64)
+        wf_scale = keep.tile([P, N], U8, align_bytes=64)
+        deal(wq_codes[:], wq_raw[:], 4)
+        deal(wq_scale[:], wq_scale_raw[:], 16)
+
+        z = [keep.tile([P, T], F32, name="z%d" % t) for t in range(PACK)]
+        for t in range(PACK):
+            for h in range(T // BANK):
+                acc = z_psum.tile([P, BANK], F32)
+                nc.tensor.matmul_mx(
+                    out=acc[:],
+                    lhsT=wq_codes[:, P * t : P * (t + 1)].bitcast(FP8X4),
+                    lhsT_scale=wq_scale[:, P * t : P * (t + 1)],
+                    rhs=xq_codes[:, 2 * BANK * h : 2 * BANK * (h + 1)].bitcast(FP4X4),
+                    rhs_scale=xq_scale[:, BANK * h : BANK * (h + 1)],
+                    start=True,
+                    stop=True,
+                )
+                nc.scalar.copy(out=z[t][:, BANK * h : BANK * (h + 1)], in_=acc[:])
+
+        old = keep.tile([P, PACK, J], F32)
+        d = keep.tile([P, PACK, J], F32)
+        for t in range(PACK):
+            nc.vector.tensor_copy(old[:, t, :], xf_planes[t][:].indirect(old_list[:]))
+            nc.vector.tensor_tensor(d[:, t, :], xf_planes[t][:].indirect(new_list[:]), old[:, t, :], subtract)
+            if t == 1:
+                deal(wf_codes[:].bitcast(U16), wf_raw[:].bitcast(U16), 8)
+                deal(wf_scale[:], wf_scale_raw[:], 16)
+
+        def interleave(engine_copy, grouped, planes):
+            engine_copy(
+                out=grouped.rearrange("p (c i) t -> p c t i", i=4),
+                in_=planes.rearrange("p t (c i) -> p c t i", i=4),
+            )
+
+        d_grouped = keep.tile([P, J, PACK], BF16, align_bytes=64)
+        d_codes = keep.tile([P, J], U32, align_bytes=64)
+        d_scale = keep.tile([P, J], U8, align_bytes=64)
+        interleave(nc.scalar.copy, d_grouped[:], d[:])
+
+        z_old = keep.tile([P, PACK, J], F32)
+        for t in range(PACK):
+            nc.vector.tensor_copy(z_old[:, t, :], z[t][:].indirect(old_list[:]))
+            if t == 2:
+                nc.vector.quantize_mx(
+                    out=d_codes[:].bitcast(FP8X4), scales=d_scale[:], in_=d_grouped[:].rearrange("p j t -> p (j t)")
+                )
+
+        y = keep.tile([P, PACK, J], F32)
+        out_rows = out_0.rearrange("(p t) j -> p t j", t=PACK)
+        for b in range(2):
+            p_acc = p_psum.tile([P, 2, J], F32, name="p_acc%d" % b)
+            for u in range(2):
+                t = 2 * b + u
+                nc.tensor.matmul_mx(
+                    out=p_acc[:, u, :],
+                    lhsT=wf_codes[:, 2 * P * t : 2 * P * (t + 1)].bitcast(FP4X4),
+                    lhsT_scale=wf_scale[:, P * t : P * (t + 1)],
+                    rhs=d_codes[:].bitcast(FP8X4),
+                    rhs_scale=d_scale[:],
+                    start=True,
+                    stop=True,
+                )
+            nc.vector.tensor_tensor(y[:, 2 * b : 2 * b + 2, :], p_acc[:], z_old[:, 2 * b : 2 * b + 2, :], add)
+            nc.sync.dma_start(out=out_rows[:, 2 * b : 2 * b + 2, :], in_=y[:, 2 * b : 2 * b + 2, :])
+
+        y_grouped = keep.tile([P, J, PACK], BF16, align_bytes=64)
+        y_codes = keep.tile([P, J], U32, align_bytes=64)
+        y_scale = keep.tile([P, J], U8, align_bytes=64)
+        interleave(nc.vector.tensor_copy, y_grouped[:], y[:])
+        nc.vector.quantize_mx(
+            out=y_codes[:].bitcast(FP8X4), scales=y_scale[:], in_=y_grouped[:].rearrange("p j t -> p (j t)")
+        )
+        nc.sync.dma_start(out=out_1[0].rearrange("p j r -> p (j r)").bitcast(I32), in_=y_codes[:].bitcast(I32))
+        for q in range(QUADS):
+            queue = nc.scalar if q % 2 == 0 else nc.sync
+            queue.dma_start(
+                out=out_2[0, 4 * q : 4 * q + 4, :].bitcast(I32),
+                in_=y_scale[32 * q : 32 * q + 4, :].bitcast(I32),
+            )

@@ -18,6 +18,7 @@ P = 128
 PACK = 4
 BANK = 512
 QUADS = 4
+HALF = J // 2
 
 
 def tile_list_change_since_lists_pl_kernel(
@@ -32,40 +33,49 @@ def tile_list_change_since_lists_pl_kernel(
         z_psum = ctx.enter_context(tc.psum_pool(name="z_psum", bufs=6))
         p_psum = ctx.enter_context(tc.psum_pool(name="p_psum", bufs=1))
 
-        def load_scale_rows(plane, rows):
-            for q in range(QUADS):
-                nc.scalar.dma_start(
+        def load_scale_rows(queues, plane, rows):
+            for q, queue in enumerate(queues):
+                queue.dma_start(
                     out=plane[32 * q : 32 * q + 4, :].bitcast(I32),
                     in_=rows[0, 4 * q : 4 * q + 4, :].bitcast(I32),
                 )
 
+        wq_scale_rows = keep.tile([P, N], U8, align_bytes=64)
         wq_scale_raw = keep.tile([P, N], U8, align_bytes=64)
         xq_scale = keep.tile([P, T], U8, align_bytes=64)
         wf_scale_raw = keep.tile([P, N], U8, align_bytes=64)
         nc.vector.memset(wq_scale_raw[:].bitcast(I32), 0)
-        nc.vector.memset(xq_scale[:].bitcast(I32), 0)
         nc.vector.memset(wf_scale_raw[:].bitcast(I32), 0)
 
         wq_raw = keep.tile([P, N], I32, align_bytes=64)
-        xq_codes = keep.tile([P, 2 * T], U8, align_bytes=64)
+        xq_codes = [
+            keep.tile([P, 2 * BANK], U8, align_bytes=64, name="xq_codes0"),
+            keep.tile([P, 2 * BANK], U8, align_bytes=64, name="xq_codes1", tag="xq_then_d"),
+        ]
         wf_raw = keep.tile([P, 2 * N], U8, align_bytes=64)
         new_list = lists.tile([P, J // 16], U16)
         old_list = lists.tile([P, J // 16], U16)
         xf_planes = [keep.tile([P, T], F32, name="xf_plane%d" % t) for t in range(PACK)]
         xf_rows = xf.rearrange("(p t) c -> p t c", t=PACK)
 
-        nc.sync.dma_start(out=wq_raw[:], in_=wq_words[0].rearrange("p n r -> p (n r)").bitcast(I32))
-        load_scale_rows(wq_scale_raw, wq_scales)
-        nc.sync.dma_start(out=xq_codes[:].bitcast(I32), in_=xq_words[0].bitcast(I32))
-        load_scale_rows(xq_scale, xq_scales)
         nc.sync.dma_start(old_list[:], offs2)
-        nc.sync.dma_start(out=xf_planes[0][:], in_=xf_rows[:, 0, :])
+        load_scale_rows((nc.sync, nc.scalar, nc.scalar, nc.scalar), wq_scale_rows, wq_scales)
         nc.sync.dma_start(new_list[:], offs)
+        nc.sync.dma_start(out=wq_raw[:], in_=wq_words[0].rearrange("p n r -> p (n r)").bitcast(I32))
+        nc.sync.dma_start(out=xf_planes[0][:], in_=xf_rows[:, 0, :])
+        nc.sync.dma_start(out=xq_codes[0][:].bitcast(I32), in_=xq_words[0, :, : 2 * BANK].bitcast(I32))
+        load_scale_rows((nc.sync,) * QUADS, xq_scale, xq_scales)
         nc.sync.dma_start(out=xf_planes[1][:], in_=xf_rows[:, 1, :])
+        nc.sync.dma_start(out=xq_codes[1][:].bitcast(I32), in_=xq_words[0, :, 2 * BANK :].bitcast(I32))
+        for t in range(2, PACK):
+            nc.sync.dma_start(out=xf_planes[t][:], in_=xf_rows[:, t, :])
         nc.sync.dma_start(out=wf_raw[:].bitcast(I32), in_=wf_words[0].bitcast(I32))
-        load_scale_rows(wf_scale_raw, wf_scales)
-        nc.sync.dma_start(out=xf_planes[2][:], in_=xf_rows[:, 2, :])
-        nc.sync.dma_start(out=xf_planes[3][:], in_=xf_rows[:, 3, :])
+        load_scale_rows((nc.sync,) * QUADS, wf_scale_raw, wf_scales)
+        for q in range(QUADS):
+            nc.vector.tensor_copy(
+                out=wq_scale_raw[32 * q : 32 * q + 4, :].bitcast(I32),
+                in_=wq_scale_rows[32 * q : 32 * q + 4, :].bitcast(I32),
+            )
 
         def deal(dealt, raw, run):
             nc.vector.tensor_copy(
@@ -81,28 +91,39 @@ def tile_list_change_since_lists_pl_kernel(
         deal(wq_scale[:], wq_scale_raw[:], 16)
 
         z = [keep.tile([P, T], F32, name="z%d" % t) for t in range(PACK)]
-        for t in range(PACK):
-            for h in range(T // BANK):
+        for h in range(T // BANK):
+            for t in range(PACK):
                 acc = z_psum.tile([P, BANK], F32)
                 nc.tensor.matmul_mx(
                     out=acc[:],
                     lhsT=wq_codes[:, P * t : P * (t + 1)].bitcast(FP8X4),
                     lhsT_scale=wq_scale[:, P * t : P * (t + 1)],
-                    rhs=xq_codes[:, 2 * BANK * h : 2 * BANK * (h + 1)].bitcast(FP4X4),
+                    rhs=xq_codes[h][:].bitcast(FP4X4),
                     rhs_scale=xq_scale[:, BANK * h : BANK * (h + 1)],
                     start=True,
                     stop=True,
                 )
                 nc.scalar.copy(out=z[t][:, BANK * h : BANK * (h + 1)], in_=acc[:])
 
-        old = keep.tile([P, PACK, J], F32)
-        d = keep.tile([P, PACK, J], F32)
+        def half(offsets, h):
+            return offsets[:, HALF // 16 * h : HALF // 16 * (h + 1)]
+
+        old = keep.tile([P, PACK, J], F32, tag="old_then_z")
+        d = [keep.tile([P, PACK, HALF], F32, name="d%d" % h) for h in range(2)]
         for t in range(PACK):
-            nc.vector.tensor_copy(old[:, t, :], xf_planes[t][:].indirect(old_list[:]))
-            nc.vector.tensor_tensor(d[:, t, :], xf_planes[t][:].indirect(new_list[:]), old[:, t, :], subtract)
-            if t == 1:
-                deal(wf_codes[:].bitcast(U16), wf_raw[:].bitcast(U16), 8)
-                deal(wf_scale[:], wf_scale_raw[:], 16)
+            for h in range(2):
+                nc.vector.tensor_copy(
+                    old[:, t, HALF * h : HALF * (h + 1)], xf_planes[t][:].indirect(half(old_list, h))
+                )
+            for h in range(2):
+                nc.vector.tensor_tensor(
+                    d[h][:, t, :],
+                    xf_planes[t][:].indirect(half(new_list, h)),
+                    old[:, t, HALF * h : HALF * (h + 1)],
+                    subtract,
+                )
+        deal(wf_codes[:].bitcast(U16), wf_raw[:].bitcast(U16), 8)
+        deal(wf_scale[:], wf_scale_raw[:], 16)
 
         def interleave(engine_copy, grouped, planes):
             engine_copy(
@@ -110,44 +131,52 @@ def tile_list_change_since_lists_pl_kernel(
                 in_=planes.rearrange("p t (c i) -> p c t i", i=4),
             )
 
-        d_grouped = keep.tile([P, J, PACK], BF16, align_bytes=64)
+        d_grouped = keep.tile([P, J, PACK], BF16, align_bytes=64, tag="xq_then_d")
         d_codes = keep.tile([P, J], U32, align_bytes=64)
         d_scale = keep.tile([P, J], U8, align_bytes=64)
-        interleave(nc.scalar.copy, d_grouped[:], d[:])
+        for h in range(2):
+            interleave(nc.scalar.copy, d_grouped[:, HALF * h : HALF * (h + 1), :], d[h][:])
 
-        z_old = keep.tile([P, PACK, J], F32)
-        for t in range(PACK):
-            nc.vector.tensor_copy(z_old[:, t, :], z[t][:].indirect(old_list[:]))
-            if t == 2:
-                nc.vector.quantize_mx(
-                    out=d_codes[:].bitcast(FP8X4), scales=d_scale[:], in_=d_grouped[:].rearrange("p j t -> p (j t)")
-                )
+        def pick_z(z_old, h):
+            for t in range(PACK):
+                nc.vector.tensor_copy(z_old[:, t, :], z[t][:].indirect(half(old_list, h)))
 
-        y = keep.tile([P, PACK, J], F32)
+        z_old0 = keep.tile([P, PACK, HALF], F32, tag="old_then_z")
+        pick_z(z_old0, 0)
+        nc.vector.quantize_mx(
+            out=d_codes[:].bitcast(FP8X4), scales=d_scale[:], in_=d_grouped[:].rearrange("p j t -> p (j t)")
+        )
+        z_old1 = keep.tile([P, PACK, HALF], F32, align_bytes=64, tag="xq_then_d")
+        pick_z(z_old1, 1)
+
         out_rows = out_0.rearrange("(p t) j -> p t j", t=PACK)
-        for b in range(2):
-            p_acc = p_psum.tile([P, 2, J], F32, name="p_acc%d" % b)
-            for u in range(2):
-                t = 2 * b + u
+        y_codes = keep.tile([P, J], U32, align_bytes=64)
+        y_scale = keep.tile([P, J], U8, align_bytes=64)
+        y_grouped = []
+        for h, z_old in enumerate((z_old0, z_old1)):
+            cols = slice(HALF * h, HALF * (h + 1))
+            p_acc = p_psum.tile([P, PACK, HALF], F32, name="p_acc%d" % h)
+            for t in range(PACK):
                 nc.tensor.matmul_mx(
-                    out=p_acc[:, u, :],
+                    out=p_acc[:, t, :],
                     lhsT=wf_codes[:, 2 * P * t : 2 * P * (t + 1)].bitcast(FP4X4),
                     lhsT_scale=wf_scale[:, P * t : P * (t + 1)],
-                    rhs=d_codes[:].bitcast(FP8X4),
-                    rhs_scale=d_scale[:],
+                    rhs=d_codes[:, cols].bitcast(FP8X4),
+                    rhs_scale=d_scale[:, cols],
                     start=True,
                     stop=True,
                 )
-            nc.vector.tensor_tensor(y[:, 2 * b : 2 * b + 2, :], p_acc[:], z_old[:, 2 * b : 2 * b + 2, :], add)
-            nc.sync.dma_start(out=out_rows[:, 2 * b : 2 * b + 2, :], in_=y[:, 2 * b : 2 * b + 2, :])
-
-        y_grouped = keep.tile([P, J, PACK], BF16, align_bytes=64)
-        y_codes = keep.tile([P, J], U32, align_bytes=64)
-        y_scale = keep.tile([P, J], U8, align_bytes=64)
-        interleave(nc.vector.tensor_copy, y_grouped[:], y[:])
-        nc.vector.quantize_mx(
-            out=y_codes[:].bitcast(FP8X4), scales=y_scale[:], in_=y_grouped[:].rearrange("p j t -> p (j t)")
-        )
+            y = keep.tile([P, PACK, HALF], F32, name="y%d" % h)
+            nc.vector.tensor_tensor(y[:], p_acc[:], z_old[:], add)
+            nc.sync.dma_start(out=out_rows[:, :, cols], in_=y[:])
+            grouped = keep.tile([P, HALF, PACK], BF16, align_bytes=64, name="y_grouped%d" % h)
+            interleave(nc.scalar.copy if h == 0 else nc.vector.tensor_copy, grouped[:], y[:])
+            y_grouped.append(grouped)
+        for h, grouped in enumerate(y_grouped):
+            cols = slice(HALF * h, HALF * (h + 1))
+            nc.vector.quantize_mx(
+                out=y_codes[:, cols].bitcast(FP8X4), scales=y_scale[:, cols], in_=grouped[:].rearrange("p j t -> p (j t)")
+            )
         nc.sync.dma_start(out=out_1[0].rearrange("p j r -> p (j r)").bitcast(I32), in_=y_codes[:].bitcast(I32))
         for q in range(QUADS):
             queue = nc.scalar if q % 2 == 0 else nc.sync

@@ -108,18 +108,18 @@ def tile_list_change_since_lists_pl_kernel(
         def half(offsets, h):
             return offsets[:, HALF // 16 * h : HALF // 16 * (h + 1)]
 
-        old = keep.tile([P, PACK, J], F32, tag="old_then_z")
-        d = [keep.tile([P, PACK, HALF], F32, name="d%d" % h) for h in range(2)]
+        old = [keep.tile([P, PACK, HALF], F32, name="old%d" % h, tag="old%d" % h) for h in range(2)]
+        d = [keep.tile([P, PACK, HALF], F32, name="d%d" % h, tag="d%d" % h) for h in range(2)]
         for t in range(PACK):
             for h in range(2):
                 nc.vector.tensor_copy(
-                    old[:, t, HALF * h : HALF * (h + 1)], xf_planes[t][:].indirect(half(old_list, h))
+                    old[h][:, t, :], xf_planes[t][:].indirect(half(old_list, h))
                 )
             for h in range(2):
                 nc.vector.tensor_tensor(
                     d[h][:, t, :],
                     xf_planes[t][:].indirect(half(new_list, h)),
-                    old[:, t, HALF * h : HALF * (h + 1)],
+                    old[h][:, t, :],
                     subtract,
                 )
         deal(wf_codes[:].bitcast(U16), wf_raw[:].bitcast(U16), 8)
@@ -141,12 +141,12 @@ def tile_list_change_since_lists_pl_kernel(
             for t in range(PACK):
                 nc.vector.tensor_copy(z_old[:, t, :], z[t][:].indirect(half(old_list, h)))
 
-        z_old0 = keep.tile([P, PACK, HALF], F32, tag="old_then_z")
+        z_old0 = keep.tile([P, PACK, HALF], F32, tag="old0")
         pick_z(z_old0, 0)
         nc.vector.quantize_mx(
             out=d_codes[:].bitcast(FP8X4), scales=d_scale[:], in_=d_grouped[:].rearrange("p j t -> p (j t)")
         )
-        z_old1 = keep.tile([P, PACK, HALF], F32, align_bytes=64, tag="xq_then_d")
+        z_old1 = keep.tile([P, PACK, HALF], F32, tag="d1")
         pick_z(z_old1, 1)
 
         out_rows = out_0.rearrange("(p t) j -> p t j", t=PACK)

from contextlib import ExitStack

import concourse.mybir as mybir

K, T, J, N = 512, 1024, 256, 512
FLOPS = 2 * K * N * (T + J)

F32 = mybir.dt.float32
BF16 = mybir.dt.bfloat16
I32 = mybir.dt.int32
U32 = mybir.dt.uint32
U16 = mybir.dt.uint16
U8 = mybir.dt.uint8
FP8X4 = mybir.dt.float8_e4m3fn_x4
FP4X4 = mybir.dt.float4_e2m1fn_x4

P = 128
PACK = 4
BANK = 512
QUADS = 4
HALF = J // 2


def tile_list_change_since_lists_pl_kernel(
    tc, xq_words, xq_scales, wq_words, wq_scales, xf, wf_words, wf_scales, offs, offs2, out_0, out_1, out_2
):
    nc = tc.nc
    add, subtract = mybir.AluOpType.add, mybir.AluOpType.subtract

    with ExitStack() as ctx:
        lists = ctx.enter_context(tc.tile_pool(name="lists", bufs=1))
        keep = ctx.enter_context(tc.tile_pool(name="keep", bufs=1))
        z_psum = ctx.enter_context(tc.psum_pool(name="z_psum", bufs=6))
        p_psum = ctx.enter_context(tc.psum_pool(name="p_psum", bufs=1))

        def load_scale_rows(queues, plane, rows):
            for q, queue in enumerate(queues):
                queue.dma_start(
                    out=plane[32 * q : 32 * q + 4, :].bitcast(I32),
                    in_=rows[0, 4 * q : 4 * q + 4, :].bitcast(I32),
                )

        wq_scale_rows = keep.tile([P, N], U8, align_bytes=64)
        wq_scale_raw = keep.tile([P, N], U8, align_bytes=64)
        xq_scale = keep.tile([P, T], U8, align_bytes=64)
        wf_scale_raw = keep.tile([P, N], U8, align_bytes=64)
        nc.vector.memset(wq_scale_raw[:].bitcast(I32), 0)
        nc.vector.memset(wf_scale_raw[:].bitcast(I32), 0)

        wq_raw = keep.tile([P, N], I32, align_bytes=64)
        xq_codes = [
            keep.tile([P, 2 * BANK], U8, align_bytes=64, name="xq_codes0"),
            keep.tile([P, 2 * BANK], U8, align_bytes=64, name="xq_codes1", tag="xq_then_d"),
        ]
        wf_raw = keep.tile([P, 2 * N], U8, align_bytes=64)
        new_list = lists.tile([P, J // 16], U16)
        old_list = lists.tile([P, J // 16], U16)
        xf_planes = [keep.tile([P, T], F32, name="xf_plane%d" % t) for t in range(PACK)]
        xf_rows = xf.rearrange("(p t) c -> p t c", t=PACK)

        nc.sync.dma_start(old_list[:], offs2)
        load_scale_rows((nc.sync, nc.scalar, nc.scalar, nc.scalar), wq_scale_rows, wq_scales)
        nc.sync.dma_start(new_list[:], offs)
        nc.sync.dma_start(out=wq_raw[:], in_=wq_words[0].rearrange("p n r -> p (n r)").bitcast(I32))
        nc.sync.dma_start(out=xf_planes[0][:], in_=xf_rows[:, 0, :])
        nc.sync.dma_start(out=xq_codes[0][:].bitcast(I32), in_=xq_words[0, :, : 2 * BANK].bitcast(I32))
        load_scale_rows((nc.sync,) * QUADS, xq_scale, xq_scales)
        nc.sync.dma_start(out=xf_planes[1][:], in_=xf_rows[:, 1, :])
        nc.sync.dma_start(out=xq_codes[1][:].bitcast(I32), in_=xq_words[0, :, 2 * BANK :].bitcast(I32))
        for t in range(2, PACK):
            nc.sync.dma_start(out=xf_planes[t][:], in_=xf_rows[:, t, :])
        nc.sync.dma_start(out=wf_raw[:].bitcast(I32), in_=wf_words[0].bitcast(I32))
        load_scale_rows((nc.sync,) * QUADS, wf_scale_raw, wf_scales)
        for q in range(QUADS):
            nc.vector.tensor_copy(
                out=wq_scale_raw[32 * q : 32 * q + 4, :].bitcast(I32),
                in_=wq_scale_rows[32 * q : 32 * q + 4, :].bitcast(I32),
            )

        def deal(dealt, raw, run):
            nc.vector.tensor_copy(
                out=dealt.rearrange("p (t c i) -> p c t i", t=PACK, i=run),
                in_=raw.rearrange("p (c i t) -> p c t i", t=PACK, i=run),
            )

        wq_codes = keep.tile([P, N], I32, align_bytes=64)
        wq_scale = keep.tile([P, N], U8, align_bytes=64)
        wf_codes = keep.tile([P, 2 * N], U8, align_bytes=64)
        wf_scale = keep.tile([P, N], U8, align_bytes=64)
        deal(wq_codes[:], wq_raw[:], 4)
        deal(wq_scale[:], wq_scale_raw[:], 16)

        z = [keep.tile([P, T], F32, name="z%d" % t) for t in range(PACK)]
        for h in range(T // BANK):
            for t in range(PACK):
                acc = z_psum.tile([P, BANK], F32)
                nc.tensor.matmul_mx(
                    out=acc[:],
                    lhsT=wq_codes[:, P * t : P * (t + 1)].bitcast(FP8X4),
                    lhsT_scale=wq_scale[:, P * t : P * (t + 1)],
                    rhs=xq_codes[h][:].bitcast(FP4X4),
                    rhs_scale=xq_scale[:, BANK * h : BANK * (h + 1)],
                    start=True,
                    stop=True,
                )
                nc.scalar.copy(out=z[t][:, BANK * h : BANK * (h + 1)], in_=acc[:])

        def half(offsets, h):
            return offsets[:, HALF // 16 * h : HALF // 16 * (h + 1)]

        old = [keep.tile([P, PACK, HALF], F32, name="old%d" % h, tag="old%d" % h) for h in range(2)]
        d = [keep.tile([P, PACK, HALF], F32, name="d%d" % h, tag="d%d" % h) for h in range(2)]
        for t in range(PACK):
            for h in range(2):
                nc.vector.tensor_copy(
                    old[h][:, t, :], xf_planes[t][:].indirect(half(old_list, h))
                )
            for h in range(2):
                nc.vector.tensor_tensor(
                    d[h][:, t, :],
                    xf_planes[t][:].indirect(half(new_list, h)),
                    old[h][:, t, :],
                    subtract,
                )
        deal(wf_codes[:].bitcast(U16), wf_raw[:].bitcast(U16), 8)
        deal(wf_scale[:], wf_scale_raw[:], 16)

        def interleave(engine_copy, grouped, planes):
            engine_copy(
                out=grouped.rearrange("p (c i) t -> p c t i", i=4),
                in_=planes.rearrange("p t (c i) -> p c t i", i=4),
            )

        d_grouped = keep.tile([P, J, PACK], BF16, align_bytes=64, tag="xq_then_d")
        d_codes = keep.tile([P, J], U32, align_bytes=64)
        d_scale = keep.tile([P, J], U8, align_bytes=64)
        for h in range(2):
            interleave(nc.scalar.copy, d_grouped[:, HALF * h : HALF * (h + 1), :], d[h][:])

        def pick_z(z_old, h):
            for t in range(PACK):
                nc.vector.tensor_copy(z_old[:, t, :], z[t][:].indirect(half(old_list, h)))

        z_old0 = keep.tile([P, PACK, HALF], F32, tag="old0")
        pick_z(z_old0, 0)
        nc.vector.quantize_mx(
            out=d_codes[:].bitcast(FP8X4), scales=d_scale[:], in_=d_grouped[:].rearrange("p j t -> p (j t)")
        )
        z_old1 = keep.tile([P, PACK, HALF], F32, tag="d1")
        pick_z(z_old1, 1)

        out_rows = out_0.rearrange("(p t) j -> p t j", t=PACK)
        y_codes = keep.tile([P, J], U32, align_bytes=64)
        y_scale = keep.tile([P, J], U8, align_bytes=64)
        y_grouped = []
        for h, z_old in enumerate((z_old0, z_old1)):
            cols = slice(HALF * h, HALF * (h + 1))
            p_acc = p_psum.tile([P, PACK, HALF], F32, name="p_acc%d" % h)
            for t in range(PACK):
                nc.tensor.matmul_mx(
                    out=p_acc[:, t, :],
                    lhsT=wf_codes[:, 2 * P * t : 2 * P * (t + 1)].bitcast(FP4X4),
                    lhsT_scale=wf_scale[:, P * t : P * (t + 1)],
                    rhs=d_codes[:, cols].bitcast(FP8X4),
                    rhs_scale=d_scale[:, cols],
                    start=True,
                    stop=True,
                )
            y = keep.tile([P, PACK, HALF], F32, name="y%d" % h)
            nc.vector.tensor_tensor(y[:], p_acc[:], z_old[:], add)
            nc.sync.dma_start(out=out_rows[:, :, cols], in_=y[:])
            grouped = keep.tile([P, HALF, PACK], BF16, align_bytes=64, name="y_grouped%d" % h)
            interleave(nc.scalar.copy if h == 0 else nc.vector.tensor_copy, grouped[:], y[:])
            y_grouped.append(grouped)
        for h, grouped in enumerate(y_grouped):
            cols = slice(HALF * h, HALF * (h + 1))
            nc.vector.quantize_mx(
                out=y_codes[:, cols].bitcast(FP8X4), scales=y_scale[:, cols], in_=grouped[:].rearrange("p j t -> p (j t)")
            )
        nc.sync.dma_start(out=out_1[0].rearrange("p j r -> p (j r)").bitcast(I32), in_=y_codes[:].bitcast(I32))
        for q in range(QUADS):
            queue = nc.scalar if q % 2 == 0 else nc.sync
            queue.dma_start(
                out=out_2[0, 4 * q : 4 * q + 4, :].bitcast(I32),
                in_=y_scale[32 * q : 32 * q + 4, :].bitcast(I32),
            )
